import numpy as np, ml_dtypes
CORES = [25,29,65,69,153,157,193,197]
N = 8
BF = ml_dtypes.bfloat16
V, L, A, T = 4096, 128, 768, 4
H = L // 2; B = V - T * H
def draw0(rng):
    ax = np.clip(np.floor(rng.random((N, 8, 1, V)) * 300 - 22 + 140 * (rng.random((N, 8, 16, V)) - 0.5)), 0, 255).astype(np.int64)
    zp = np.clip(np.floor(rng.random((N, 8, 1, A)) * 170 + 40 + 160 * (rng.random((N, 8, 16, A)) - 0.5)), 0, 255).astype(np.int64)
    p = np.clip(np.floor(rng.random((N, 8, 1, L)) * 130 + 60 + 160 * (rng.random((N, 8, 16, L)) - 0.5)), 0, 255).astype(np.int64)
    near = (rng.random((N, 8, 1, H)) < 0.6) & (rng.random((N, 8, 16, H)) > 0.15)
    p[..., 1::2] = np.where(near, p[..., ::2], p[..., 1::2])
    rt = rng.integers(0, V, (N, 8, 16, A)); ex = rng.integers(0, V, (N, 8, 16, L))
    ex[..., 1::2] = np.where(rng.random((N, 8, 16, H)) < 0.2, ex[:, :, ::-1, ::2], ex[..., 1::2])
    return ax, rt, zp, ex, p, rng.integers(0, 4096, (N, 8, 16)), rng.integers(0, 4096, (N, 8, 16))
def pack(ax, rt, zp, ex, p, wt, km):
    b = lambda a: np.ascontiguousarray(a.reshape(N, 128, -1)).astype(np.float32).astype(BF)
    w = lambda a: np.ascontiguousarray(a.reshape(N, 128, -1)).astype(np.int32)
    return {"ax": b(ax), "rt": w(rt), "zp": b(zp), "ex": w(ex), "p0": b(p), "wt": w(wt), "km": w(km)}
def setup_inputs(rng):
    return pack(*draw0(rng))
def setup_inputs_spread(rng):
    def uneven(n): return np.minimum(np.floor(np.exp2(1 + 7.3 * rng.random((N, 8, 1, n))) * rng.random((N, 8, 16, n))), 255).astype(np.int64)
    ax, zp, p = uneven(V), uneven(A), uneven(L)
    p[..., 1::2] = np.where(rng.random((N, 8, 1, H)) < 0.4, p[..., ::2], p[..., 1::2])
    rt = np.minimum(np.floor(V * rng.random((N, 8, 16, A)) ** (0.5 + 3 * rng.random((N, 8, 1, A)))), V - 1).astype(np.int64)
    ex = np.minimum(np.floor(V * rng.random((N, 8, 16, L)) ** (0.5 + 3 * rng.random((N, 8, 1, L)))), V - 1).astype(np.int64)
    wt = np.minimum(np.floor(np.exp2(12.1 * rng.random((N, 8, 16)))) - 1, 4095).astype(np.int64)
    km = np.minimum(np.floor(np.exp2(12.1 * rng.random((N, 8, 16)))) - 1, 4095).astype(np.int64)
    return pack(ax, rt, zp, ex, p, wt, km)
def setup_inputs_ends(rng):
    den = np.array([0.0, 0.1, 0.25, 0.5, 0.75, 1.0])
    ax = 255 * (rng.random((N, 8, 16, V)) < rng.choice(den, (N, 8, 1, V))); zp = 255 * (rng.random((N, 8, 16, A)) < rng.choice(den, (N, 8, 1, A)))
    p = 255 * (rng.random((N, 8, 16, L)) < rng.choice(np.array([0.0, 0.25, 0.5, 0.75, 0.9, 1.0]), (N, 8, 1, L)))
    p[..., 1::2] = np.where(rng.random((N, 8, 1, H)) < 0.5, p[..., ::2], p[..., 1::2])
    for g, (a, b) in enumerate(((0.0, 0.4), (0.2, 1.0), (0.3, 0.7), (0.4, 0.0), (0.5, 0.3), (0.7, 0.2), (1.0, 0.3), (0.3, 0.5))):
        ax[:, g, :, 0] = 255 * (rng.random((N, 16)) < a); ax[:, g, :, V - 1] = 255 * (rng.random((N, 16)) < b)
    def names(n): return np.where(rng.random((N, 8, 16, n)) < 0.85, (V - 1) * rng.integers(0, 2, (N, 8, 16, n)), rng.integers(0, V, (N, 8, 16, n)))
    rt, ex = names(A), names(L)
    wt = 4095 * rng.integers(0, 2, (N, 8, 16)); km = 4095 * rng.integers(0, 2, (N, 8, 16))
    wt[:, 7] = 4095; wt[:, 5:7, 15] = 4095; wt[:, 0, 0] = 0; wt[:, 0, 1] = 4095
    for m, k in ((0, 0), (1, 4095), (3, 8), (9, 3856), (15, 3841)): km[:, 5:, m] = k
    one = np.zeros(16, np.int64); one[15] = 1
    for i in (0, 1, L - 2, L - 1): p[:, 5:, :, i] = one
    for i in (2, 3, L - 4, L - 3): p[:, 7, :, i] = 255; p[:, 6, :, i] = 0
    p[N - 1, 7, :, L - 2:] = 255
    for h in (3840, 3841, 4095, 4080, 3832): zp[:, 5:, :, (h * A) >> 12] = 255
    zp[:, 6, :, (4080 * A) >> 12] = 0; zp[:, 6, :, (4095 * A) >> 12] = 0; zp[:, 5, :, (4095 * A) >> 12] = 0
    for h in (8, 4088, 24, 264, 136): zp[:, 7, :, (h * A) >> 12] = 0
    zp[:, 6, :, 0] = 255
    return pack(ax, rt, zp, ex, p, wt, km)
def setup_inputs_corners(rng):
    ax, rt, zp, ex, p, wt, km = draw0(rng)
    cnt = rng.integers(0, 17, (N, 8, 1, V)); cnt[..., :17] = np.arange(17)
    hi = ((np.arange(16)[:, None] + rng.integers(0, 16, (N, 8, 1, V))) & 15) < cnt
    ax = np.where(hi, rng.integers(139, 256, ax.shape), rng.integers(0, 111, ax.shape))
    p = rng.integers(111, 140, p.shape); p[..., 1::2] = np.where(rng.random((N, 8, 1, H)) < 0.5, p[..., ::2], p[..., 1::2])
    sets = ((0, 1, 2, 3), (9, 10, 12, 16), (3, 4), (4, 5, 6, 7, 8), (8, 9), tuple(range(17)), (8,), ())
    full = int(rng.integers(0, N))
    for q in range(N):
        for g in range(8):
            s = 0 if q == full else (q + g) & 7
            cand = np.flatnonzero(np.isin(cnt[q, g, 0], np.array(sets[s], np.int64))) if s < 7 else np.array([0, B - 1, B, B + H - 1, B + H, V - 2, V - 1])
            if s == 6: cand = cand[:1]
            rt[q, g] = cand[rng.integers(0, len(cand), (16, A))]
    nm = (rng.integers(0, V, (N, 8, 1, H)) + (2 * rng.integers(0, V // 2, (N, 8, 1, H)) + 1) * np.arange(32)[:, None]) & (V - 1)
    ea, eb = nm[:, :, :16], nm[:, :, 16:]; rep = np.broadcast_to(nm[:, :, :1], ea.shape)
    kd = (np.arange(H)[None, None, None, :] + np.arange(8)[None, :, None, None] + np.arange(N)[:, None, None, None]) % 6
    lone = eb.copy(); lone[:, :, 0] = ea[:, :, 15]
    ex[..., ::2] = np.where(kd >= 4, rep, ea)
    ex[..., 1::2] = np.where(kd == 0, ea, np.where(kd == 1, ea[:, :, ::-1], np.where(kd == 3, lone, np.where(kd == 4, rep, eb))))
    ch = rng.integers(0, 3, (N, 8, 1, A)); ch[:, 1] = 0
    zp = np.take_along_axis(rng.integers(0, 256, (N, 8, 16, 3)), ch, 3)
    km[:, 2] = rng.integers(0, 4096, (N, 1)); km[:, 3, ::2] = 0; km[:, 3, 1::2] = 4095; wt[:, 4] = 0; wt[:, 6, 1:] = 0; wt[:, 6, 0] = 4095
    return pack(ax, rt, zp, ex, p, wt, km)
def setup_inputs_alike(rng):
    ax, rt, zp, ex, p, wt, km = draw0(rng)
    p[:, ::2] = p[:, ::2, :, :1]
    p[:, 1::2] = np.take_along_axis(p[:, 1::2, :, :4], rng.integers(0, 4, (N, 4, 1, L)), 3)
    rt = np.take_along_axis(rt[..., :8], rng.integers(0, 8, (N, 8, 1, A)), 3)
    rt[:, 3] = rng.choice(np.array([0, V - 1, B, B - 1]), (N, 16, A))
    ex[:, ::2] = rng.choice(np.array([0, 5, B - 1, B, B + H, V - 1]), (N, 4, 16, L))
    zp[:, 4:] = np.take_along_axis(zp[:, 4:, :, :16], rng.integers(0, 16, (N, 4, 1, A)), 3)
    wt[:, 5, :14] = rng.integers(3200, 4096, (N, 14)); wt[:, 5, 14] = 256; wt[:, 5, 15] = 1
    aim = np.array([0, 4095, 4075, 4077, 4087])[np.arange(H // 2) % 5]
    big = rng.integers(200, 256, (N, 14, H // 2))
    rest = (4096 + aim - np.sum(wt[:, 5, :14, None] * big, axis=1)) & 8191
    p[:, 5, :14, 2::4] = big; p[:, 5, 14, 2::4] = rest >> 8; p[:, 5, 15, 2::4] = rest & 255; p[:, 5, :, 3::4] = 0
    for k, v in ((5, V - 3), (6, V - 5), (7, V - 7)):
        rt[:, 5, k] = v; ax[:, 5, :, v] = 0; ax[:, 5, :4, v] = 255; ax[:, 5, 14:, v] = 255
    for v, u in ((V - 3, 4075), (V - 5, 4077), (V - 7, 4087), (V - 3, 4095), (V - 3, 4096)): ax[:, 5, :, (((v * u) >> 5) + v) & (V - 1)] = 255
    return pack(ax, rt, zp, ex, p, wt, km)
def check_inputs(d):
    bad = []
    for k, hi in (("ax", 255), ("rt", V - 1), ("zp", 255), ("ex", V - 1), ("p0", 255), ("wt", 4095), ("km", 4095)):
        v = np.asarray(d[k]).astype(np.float64)
        if not (np.min(v) >= 0 and np.max(v) <= hi): bad.append("range of " + k)
        elif np.any(v != np.floor(v)): bad.append("whole numbers of " + k)
    return bad
def pick(x, e):
    n = e.shape[3]
    return np.take_along_axis(x, e.reshape(N, 8, 1, 16 * n), 3).reshape(N, 8, 16, 16, n)
def reference(ax, rt, zp, ex, p0, wt, km):
    x = ax.astype(np.float32).astype(np.int64).reshape(N, 8, 16, V)
    r = np.zeros((N, 8, 16, A + T * L), np.int64); z = np.zeros((N, 8, 16, A + T * L), np.int64)
    r[..., :A] = rt.reshape(N, 8, 16, A); z[..., :A] = zp.astype(np.float32).astype(np.int64).reshape(N, 8, 16, A)
    e0 = ex.astype(np.int64).reshape(N, 8, 16, L); p = p0.astype(np.float32).astype(np.int64).reshape(N, 8, 16, L)
    w = wt.astype(np.int64).reshape(N, 8, 16, 1); k = km.astype(np.int64).reshape(N, 8, 16, 1); odd = np.zeros(N, np.int64)
    for t in range(T):
        n = A + L * t
        u = np.repeat(np.add.reduce(w * p, axis=2)[:, :, ::2] & 4095, 2, axis=2)[:, :, None, :]
        c = (((((u * u) >> 5) & 4095) + ((k * u) & 4095)) & 4095) * n >> 12
        score = np.sum(np.abs(pick(z, c) - p[:, :, :, None, :]), axis=2)
        a = np.minimum.reduce(score * 4096 + c, axis=2) & 4095
        e = np.take_along_axis(r, a[:, :, None, :], 3)
        v = np.sum(pick(x, e) >= p[:, :, :, None, :], axis=2)
        barred = v < 4 + odd[:, None, None, None]
        e2 = (((e * u) >> 5) + e + 77 * t) & (V - 1)
        v2 = np.sum(pick(x, e2) >= p[:, :, :, None, :], axis=2)
        f = np.where(barred, e0, np.where((v < 9) & (v2 >= v), e2, e))
        odd = np.sum(barred, axis=(1, 2, 3)) & 1
        fa, fb = f[..., ::2].copy(), f[..., 1::2].copy()
        same = fa[:, :, :, None, :] == fb[:, :, None, :, :]
        ca, cb = np.any(same, axis=3), np.any(same, axis=2)
        rec = np.maximum.reduce(np.where(ca[:, :, None], pick(x, fa), 0), axis=3)
        new = B + H * t + np.arange(H)
        f[..., ::2] = np.where(ca, new, fa); f[..., 1::2] = np.where(cb, new, fb)
        src = (np.arange(N) - 1 - t % 3) % N
        f, p = f[src], p[src]
        r[..., n:n + L] = f
        if t < T - 1: z[..., n:n + L] = p
        x[..., B + H * t:B + H * t + H] = rec[src]
        p = (p + 255 - np.take_along_axis(x, f[:, :, :1], 3)) >> 1
    return {"yr": r[..., A:].reshape(N, 128, T * L).astype(np.float32), "yp": p.reshape(N, 128, L).astype(np.float32)}

from concourse.mybir import AluOpType as A, ActivationFunctionType as F

LV = 76
QS = 44
_D = {"f": "float32", "b": "bfloat16", "h": "float16", "i": "int32", "u": "uint16"}
_S = """XT 4112 b;RW 1280 f;ZW 1280 b;RI 768 i;EI 128 i;E128 128 f;WI 16 i;WI2 16 i;KI 16 i;COL 16 f;PI 128 b;PN 512 b;P 128 b;PT 128 b
PRS 2048 b;PB 128 f;IP 4 i;IOT 128 f;R16 128 f;G16 128 f;NEW 256 f;KLI 8 i;KL 8 u;I 128 b;IPM 128 b;EX 2048 b;BB 128 b;NB 128 b
B4 8 b;B8 8 b;B8F 8 f;B8H 8 h;IH 128 h;I8 128 b;MASK 128 f;RST 128 f;RQ 1024 b;ONESF 128 f;SEL 2048 b;BC 2048 h;WH 128 b;WL 128 b
BAR 1 f;UI 64 i;UM 64 i;SQ 64 i;T1 64 i;H1 64 i;H2 64 i;C16 64 u;CF 64 h;ZG 1024 b;AB 2048 b;SC 128 f;LM 128 f;LI 8 i;LA 8 i;L16 8 u
E16 128 u;EF 128 f;EFS 128 f;EU 128 i;SH 128 i;SM 128 i;SA 128 i;E216 128 u;VB 2048 b;VB2 2048 b;XG 1024 b;XG2 1024 b;VT 128 b;VT2 128 b
BR 128 f;G9 128 f;TH2 128 f;BAS 128 f;BASC 128 f;JNK 128 f;CNT 1 f;CI 2 i;FC 128 h;FF 128 f;FQ 64 f;EQ 1024 b;Q16 64 u;GQ 1024 b
SQM 1024 b;FL 128 f;FH 128 h;FM 128 h;FS 512 f;MS 288 u;ML 288 u;AF 128 h;YP 128 f;relp 512 b;relf 512 f;relm 288 u"""
SCRATCH = {x.split()[0]: ("sbuf", [128, int(x.split()[1])], _D[x.split()[2]]) for x in _S.replace("\n", ";").split(";")}
WID = {k: v[1][1] for k, v in SCRATCH.items()}
for _b in range(8):
    SCRATCH["pb%d" % _b] = ("psum", [128, 512], "float32")
SEMAPHORES = (["sv", "sa", "st", "sg", "ls", "rl", "lp", "lw", "lk", "lz", "lr", "le", "lx0", "lx1", "o0", "o1", "o2"]
              + ["a%s%d" % (k, t) for k in "pfm" for t in range(4)])
N = 8


def nxt(r, t):
    return (r + 1 + t % 3) % N


def hops(T, topo, src, dst, kind):
    if topo.may_write(src, dst):
        return [dst]
    c = [x for x in topo.cores_of(src) if topo.die(x) == topo.die(src) and topo.may_write(x, dst) and T.rank_of(x) is None]
    return [c[0] if kind == "f" else c[-1], dst]


def send(g, topo, src, dst, out, in_, rsem, lsem):
    rid, pid = topo.addr(dst, src)
    g.remote_dma(out, in_, rsem, lsem, pid, rid, topo.mask(src, dst))
    return len(topo.engines(src, dst))


def final_place(T, kind, t):
    n = 768 + 128 * t
    if kind == "p":
        return T.ZW[:, n:n + 128], T.relp[:, 128 * t:128 * t + 128]
    if kind == "f":
        return T.RW[:, n:n + 128], T.relf[:, 128 * t:128 * t + 128]
    return T.ML[:, 72 * t:72 * t + 72], T.relm[:, 72 * t:72 * t + 72]


def relay_program(g, core, T, topo):
    sent = 0
    for t in range(4):
        for kind in "pmf":
            for r in range(N):
                src, dst = T.cores[r], T.cores[nxt(r, t)]
                h = hops(T, topo, src, dst, kind)
                if len(h) < 2 or h[0] != core:
                    continue
                sem = T.sem["a%s%d" % (kind, t)]
                g.wait_ge(sem, len(topo.engines(src, core)))
                a, b = final_place(T, kind, t)
                sent += send(g, topo, core, dst, a, b, sem, T.sem.rl)
    if sent:
        g.wait_ge(T.sem.rl, sent)


def rank_program(g, core, T, topo):
    rank = T.rank_of(core)
    if rank is None:
        relay_program(g, core, T, topo)
        return
    eng = {"V": g.vector, "S": g.scalar, "T": g.tensor, "G": g, "Y": g.sync}
    own = {"V": "sv", "S": "sa", "T": "st", "G": "sg"}
    total, acc, clk, evc = {}, {}, {q: {} for q in eng}, {}

    def merge(a, b):
        for s, c in b.items():
            if a.get(s, 0) < c:
                a[s] = c

    def note(buf, lo, hi, st, isw, sem, cnt, q):
        keep = [x for x in acc.get(buf, []) if not (isw and st == 1 and lo <= x[0] and x[1] <= hi) and x[:5] != (lo, hi, st, isw, sem)]
        acc[buf] = keep + [(lo, hi, st, isw, sem, cnt, q)]

    def waits(q, regs):
        need = {}
        for buf, lo, hi, st, isw in regs:
            ps = buf[:2] == "pb"
            for lo2, hi2, st2, w2, sem, cnt, q2 in acc.get(buf, []):
                if hi2 <= lo or hi <= lo2 or (st == st2 > 1 and (lo - lo2) % st):
                    continue
                if q2 == q and own.get(q) == sem:
                    if not w2 or (q == "T" and isw):
                        continue
                elif not (isw or w2 or (ps and q2 != q)):
                    continue
                if clk[q].get(sem, 0) < cnt and need.get(sem, 0) < cnt:
                    need[sem] = cnt
        for s in sorted(need):
            c = need[s]
            if clk[q].get(s, 0) >= c or any(s2 != s and evc[(s2, c2)].get(s, 0) >= c for s2, c2 in need.items()):
                continue
            eng[q].wait_ge(T.sem[s], c)
            merge(clk[q], evc[(s, c)])
        for s, c in need.items():
            merge(clk[q], evc[(s, c)])

    def regions(reads, writes):
        out = []
        for isw, xs in ((False, reads), (True, writes)):
            for x in xs:
                for r in x[1]:
                    out.append(((r[0], 0, 512, 1) if r[0][:2] == "pb" else r) + (isw,))
        return out

    def op(q, make, writes, reads, sem=None, inc=1):
        regs = regions(reads, writes)
        waits(q, regs)
        sem = sem or own[q]
        make(eng[q]).then_inc(T.sem[sem], inc)
        total[sem] = total.get(sem, 0) + inc
        c = dict(clk[q])
        c[sem] = total[sem]
        evc[(sem, total[sem])] = c
        for r in regs:
            note(*r, sem, total[sem], q if inc == 1 else "D")

    def b(name, lo=0, hi=None, st=1, p=128, p0=0):
        hi = WID.get(name, 128) if hi is None else hi
        return (T[name][p0:p, lo:hi:st], [(name, lo, hi, st)])

    def ind(w, o): return (w[0].indirect(o[0]), w[1] + o[1])
    def ts(out, a, s1, s2, o0, o1=None):
        ins = [a]
        if isinstance(s1, tuple):
            ins.append(s1)
            s1 = s1[0]
        if o1 is None:
            op("V", lambda e: e.tensor_scalar(out[0], a[0], s1, s2, o0), [out], ins)
        else:
            op("V", lambda e: e.tensor_scalar(out[0], a[0], s1, s2, o0, o1), [out], ins)
    def tt(out, a, c, o): op("V", lambda e: e.tensor_tensor(out[0], a[0], c[0], o), [out], [a, c])
    def cp(out, a): op("V", lambda e: e.tensor_copy(out[0], a[0]), [out], [a])
    def ms(out, c): op("V", lambda e: e.memset(out[0], c), [out], [])
    def scan(out, a, c, o0, o1): op("V", lambda e: e.tensor_tensor_scan(out[0], a[0], c[0], 0.0, o0, o1), [out], [a, c])
    def act(out, a, f=F.Copy, bias=0.0, scale=1.0, accum=None):
        ins, outs = [a], [out]
        kw = {"bias": bias, "scale": scale}
        for k in kw:
            if isinstance(kw[k], tuple):
                ins.append(kw[k])
                kw[k] = kw[k][0]
        if accum is not None:
            outs.append(accum)
            kw["accum_out"] = accum[0]
        op("S", lambda e: e.activation(out[0], a[0], f, **kw), outs, ins)
    def mm(out, l, r, start=True, stop=True): op("T", lambda e: e.matmul(out[0], l[0], r[0], start, stop), [out], [l, r])
    def dma(q, sem, out, in_, w, r): op(q, lambda e: e.dma_start(out, in_), w, r, sem, 16)
    def iota(out, pat, base, cm, small=True):
        if small:
            op("G", lambda e: e.iota(out[0], pat, base, cm, allow_small_or_imprecise_dtypes=True), [out], [])
        else:
            op("G", lambda e: e.iota(out[0], pat, base, cm), [out], [])

    sent = [0]
    def push(kind, t, x):
        waits("G", regions([x], []))
        dst = T.cores[nxt(rank, t)]
        h = hops(T, topo, core, dst, kind)
        sent[0] += send(g, topo, core, h[0], final_place(T, kind, t)[len(h) - 1], x[0], T.sem["a%s%d" % (kind, t)], T.sem.ls)
    def arrive(kind, t, x):
        src = T.cores[(rank - 1 - t % 3) % N]
        h = [src] + hops(T, topo, src, core, kind)
        sem, cnt = "a%s%d" % (kind, t), len(topo.engines(h[-2], core))
        total[sem] = cnt
        evc[(sem, cnt)] = {sem: cnt}
        note(*x[1][0], True, sem, cnt, "D")

    dma("Y", "lp", T.PI[:], T.p0[:], [b("PI")], [])
    dma("S", "lw", T.WI[:, 0:1], T.wt[:], [b("WI")], [])
    dma("Y", "lk", T.KI[:, 0:1], T.km[:], [b("KI")], [])
    dma("S", "lz", T.ZW[:, 0:768], T.zp[:], [b("ZW", 0, 768)], [])
    dma("Y", "lr", T.RI[:], T.rt[:], [b("RI")], [])
    dma("S", "lx0", T.XT[:, 16:2064], T.ax[:, 0:2048], [b("XT", 16, 2064)], [])
    dma("Y", "lx1", T.XT[:, 2064:4112], T.ax[:, 2048:4096], [b("XT", 2064, 4112)], [])
    dma("Y", "le", T.EI[:], T.ex[:], [b("EI")], [])
    C = lambda j: b("COL", j, j + 1)
    IP = lambda j: b("IP", j, j + 1)
    iota(IP(0), [[0, 1]], 0, 1, False)
    iota(b("IOT"), [[1, 128]], 0, 0)
    iota(b("G16"), [[1, 8], [0, 16]], 0, 0)
    iota(b("KLI"), [[16, 8]], 15, 0, False)
    iota(b("R16"), [[0, 8], [1, 16]], 0, 0)
    push("p", 0, b("PI"))
    iota(b("NEW"), [[1, 256]], 3840, 0)
    ms(b("RST"), -1.0e9)
    ms(b("SEL"), 0.0)
    ms(b("BAR"), 4.0)
    ms(b("XT", 0, 16), 0.0)
    ms(b("RST", 0, 128, 16), 1.0e9)
    ts(IP(1), IP(0), 15, None, A.bitwise_and)
    ts(IP(2), IP(0), 4, None, A.arith_shift_right)
    for j in range(3):
        cp(C(j), IP(j))
    ts(b("I"), b("IOT"), C(0), None, A.is_equal)
    ts(b("IPM", 0, 64), b("IOT", 0, 64), C(0), None, A.is_equal)
    ts(b("IPM", 64, 128), b("IOT", 64, 128), C(0), -1.0, A.is_equal, A.mult)
    ts(b("BB"), b("G16"), C(2), None, A.is_equal)
    for m in range(16):
        cp(b("EX", m, 2048, 16), b("IPM"))
    for h in range(2):
        cp(b("P", 64 * h, 64 * h + 64), b("PI", h, 128, 2))
    ts(b("WI2", 0, 1), b("WI", 0, 1), 6, None, A.arith_shift_right)
    ts(b("WI2", 1, 2), b("WI", 0, 1), 63, None, A.bitwise_and)
    cp(C(6), b("KI", 0, 1))
    for j in range(2):
        cp(C(4 + j), b("WI2", j, j + 1))
    ts(b("WH"), b("BB"), C(4), 64.0, A.mult, A.mult)
    ts(b("WL"), b("BB"), C(5), None, A.mult)
    ts(b("NB"), b("BB"), -2048.0, None, A.mult)
    ts(b("B4"), b("BB", 0, 128, 16), 4096.0, None, A.mult)
    cp(b("B8F"), b("BB", 0, 128, 16))
    cp(b("B8"), b("BB", 0, 128, 16))
    cp(b("IH"), b("I"))
    ts(b("MASK"), b("R16"), C(1), None, A.is_equal)
    cp(b("KL"), b("KLI"))

    W0, W1, W2 = 16 * LV, min(16 * LV + 512, 2048), 2048
    parts = [(W0, W1)] + ([(W1, W2)] if W2 > W1 else [])
    XW, XQ = b("XT", 16, 4112), b("XT")
    for t in range(4):
        n = 768 + 128 * t
        lane = lambda buf, h: b(buf, 128 * t + h, 128 * t + 128, 2)
        half = lambda buf, h: b(buf, 64 * h, 64 * h + 64)
        mm(b("pb5", 0, 64), b("WH"), half("P", 0), True, False)
        mm(b("pb5", 0, 64), b("WL"), half("P", 0), False, True)
        mm(b("pb7"), b("P"), b("I"))
        act(b("PT"), b("pb7"))
        for k in (2, 3, 0, 1):
            mm(b("pb%d" % k, 0, 512), b("PT"), b("EX", 512 * k, 512 * k + 512), True, k < 2)
        if t:
            for h in range(2):
                act(lane("PN", h), half("P", h))
            push("p", t, b("PN", 128 * t, 128 * t + 128))
        cp(b("UI"), b("pb5", 0, 64))
        ts(b("UM"), b("UI"), 4095, None, A.bitwise_and)
        tt(b("SQ"), b("UM"), b("UM"), A.mult)
        ts(b("pb5", 64, 128), b("UM"), C(6), None, A.mult)
        ts(b("T1"), b("SQ"), 5, 4095, A.arith_shift_right, A.bitwise_and)
        tt(b("H1"), b("T1"), b("pb5", 64, 128), A.add)
        ts(b("H2"), b("H1"), 4095, None, A.bitwise_and)
        ts(b("C16"), b("H2"), n / 4096.0, -31.0 / 64.0, A.mult, A.add)
        act(b("ZG", 512, 1024), ind(b("ZW", 0, n), b("C16", 32, 64)))
        cp(b("ZG", 0, 512), ind(b("ZW", 0, n), b("C16", 0, 32)))
        cp(b("CF"), b("C16"))
        for h in range(2):
            cp(b("pb5", 128 + 64 * h, 192 + 64 * h), b("UM"))
        for k in (0, 1):
            z = b("ZG", 512 * k, 512 * k + 512)
            mm(b("pb%d" % (2 + k), 0, 512), b("I"), z, False, True)
            tt(b("AB", 512 * k, 512 * k + 512), z, b("pb%d" % k, 0, 512), A.max)
            act(b("AB", 1024 + 512 * k, 1536 + 512 * k), b("pb%d" % (2 + k), 0, 512), F.Abs, scale=0.5)
        mm(b("pb4"), b("P"), b("NB"), True, False)
        for m in range(16):
            mm(b("pb4", m, 128, 16, 64), b("ZG", m, 1024, 16), b("NB", 0, 128, 16), False, False)
        for h in range(2):
            mm(b("pb4", p0=64 * h, p=64 * h + 64), b("CF"), b("IH"), False, False)
        if LV > 64:
            mm(b("pb6", 0, W0 - 1024), b("PT"), b("EX", 1024, W0))
        for m in range(16):
            mm(b("pb4", m, 128, 16), b("AB", m, 2048, 16), b("B4"), False, m == 15)
        for k in (0, 1):
            act(b("PRS", 512 * k, 512 * k + 512), b("pb%d" % k, 0, 512))
        if LV > 64:
            act(b("PRS", 1024, W0), b("pb6", 0, W0 - 1024), scale=-1.0)
        if t == 0:
            cp(b("RW", 0, 768), b("RI"))
            for k in range(16):
                cp(b("SEL", 128 * k + k, 128 * k + 128, 16), b("B8"))
        scan(b("SC"), b("RST"), b("pb4"), A.max, A.min)
        tt(b("LM"), ind(b("SC"), b("KL")), b("MASK"), A.mult)
        mm(b("pb4", 128, 136), b("LM"), b("B8F"))
        cp(b("LI"), b("pb4", 128, 136))
        ts(b("LA"), b("LI"), 2047, None, A.bitwise_and)
        cp(b("L16"), b("LA"))
        act(b("EF"), ind(b("RW", 0, n), b("L16")))
        cp(b("E16"), ind(b("RW", 0, n), b("L16")))
        act(b("pb7"), b("EF"), bias=77.0 * t)
        tt(b("EU"), b("EF"), b("pb5", 128, 256), A.mult)
        ts(b("SH"), b("EU"), 5, None, A.arith_shift_right)
        tt(b("SM"), b("SH"), b("pb7"), A.add)
        ts(b("SA"), b("SM"), 4095, None, A.bitwise_and)
        cp(b("E216"), b("SA"))
        for k in (2, 0):
            for i, (lo, hi) in enumerate(parts):
                mm(b("pb%d" % (k + i), 0, hi - lo), b("PT"), b("EX", lo, hi), True, False)
        sets = (("E16", "XG", "VB", "VT", 2, 6), ("E216", "XG2", "VB2", "VT2", 0, 7))
        for lst, xg, vb, vt, k, c in sets:
            act(b(xg, 0, W2 - W0), ind(XW, b(lst, LV, 128)))
            tt(b(vb, 0, W0), ind(XW, b(lst, 0, LV)), b("PRS", 0, W0), A.is_ge)
            for i, (lo, hi) in enumerate(parts):
                mm(b("pb%d" % (k + i), 0, hi - lo), b("I"), b(xg, lo - W0, hi - W0), False, True)
        for lst, xg, vb, vt, k, c in sets:
            for i, (lo, hi) in enumerate(parts):
                act(b(vb, lo, hi), b("pb%d" % (k + i), 0, hi - lo), F.Sign, bias=0.5)
        for lst, xg, vb, vt, k, c in sets:
            if t == 0 and c == 6:
                ts(C(8), C(0), LV - 0.5, -0.5, A.is_ge, A.mult)
                ts(C(9), C(8), 1.0, None, A.add)
                ts(C(10), C(8), -16.0, None, A.mult)
            for m in range(16):
                mm(b("pb%d" % c, m, 128, 16), b(vb, m, 2048, 16), b("B8"))
            act(b(vt), b("pb%d" % c), F.Identity, C(10), C(9))
            mm(b("pb%d" % c), b(vt), b("I"))
        act(b("EFS"), b("EF"), scale=1.0 / 128.0)
        if t == 0:
            for h in range(2):
                ts(half("E128", h), b("EI", h, 128, 2), 1.0 / 128.0, None, A.mult)
            for k in range(16):
                ts(b("BC", 128 * k, 128 * k + 128), b("BB"), b("MASK", k, k + 1), None, A.mult)
            cp(b("B8H"), b("BB", 0, 128, 16))
            ts(b("I8"), b("I"), 8192.0, None, A.mult)
            ms(b("ONESF"), 1.0)
            ms(b("RQ"), 255.0)
            ms(b("RQ", 0, 1024, 16), 0.0)
        tt(b("pb5", 256, 384), b("SA"), b("EF"), A.subtract)
        tt(b("pb5", 384, 512), b("E128"), b("EFS"), A.subtract)
        ts(b("BR"), b("pb6"), b("BAR"), 128.0, A.is_lt, A.mult)
        ts(b("G9"), b("pb6"), 9.0, 128.0, A.is_ge, A.mult)
        tt(b("pb5", 384, 512), b("BR"), b("pb5", 384, 512), A.mult)
        tt(b("pb6"), b("G9"), b("pb6"), A.max)
        tt(b("BAS"), b("EF"), b("pb5", 384, 512), A.add)
        tt(b("TH2"), b("BR"), b("pb6"), A.max)
        act(b("BASC"), b("BAS"), bias=-2048.0)
        if t < 3:
            act(b("JNK"), b("BR"), scale=1.0 / 128.0, accum=b("CNT"))
        tt(b("FL"), b("pb7"), b("TH2"), A.is_ge)
        tt(b("pb5"), b("FL"), b("pb5", 256, 384), A.mult)
        tt(b("FC"), b("BASC"), b("pb5"), A.add)
        tt(b("FF"), b("BAS"), b("pb5"), A.add)
        act(b("FQ"), half("FF", 0), bias=16.0)
        for k in range(16):
            mm(b("pb%d" % (k // 4), 64 * (k % 4), 64 * (k % 4) + 64), b("BC", 128 * k, 128 * k + 128), half("FC", 1))
        for k in range(16):
            tt(half("EQ", k), half("FC", 0), b("pb%d" % (k // 4), 64 * (k % 4), 64 * (k % 4) + 64), A.is_equal)
            mm(b("pb4", 0, 64), b("I8"), half("EQ", k), k == 0, k == 15)
        for k in range(16):
            mm(b("pb6", 0, 64), b("SEL", 128 * k, 128 * k + 128), half("EQ", k), k == 0, k == 15)
        for h in range(2):
            tt(b("pb5", 256 + 64 * h, 320 + 64 * h), b("NEW", 64 * t, 64 * t + 64), half("FF", h), A.subtract)
        tt(b("Q16"), b("FQ"), b("pb4", 0, 64), A.min)
        act(b("GQ", 0, 16 * QS), ind(XQ, b("Q16", 0, QS)))
        cp(b("GQ", 16 * QS, 1024), ind(XQ, b("Q16", QS, 64)))
        for h, k in ((0, 4), (1, 6)):
            ts(half("FL", h), b("pb%d" % k, 0, 64), 0.5, None, A.is_ge)
        tt(b("pb5"), b("FL"), b("pb5", 256, 384), A.mult)
        tt(b("FH"), b("FC"), b("pb5"), A.add)
        mm(b("pb7"), b("FH"), b("BC", 0, 128))
        scan(b("SQM", 16 * QS, 1024), b("RQ", 16 * QS, 1024), b("GQ", 16 * QS, 1024), A.min, A.max)
        tt(b("FM"), b("MASK"), b("pb7"), A.mult)
        mm(b("pb7", 256, 264), b("FM"), b("B8H"))
        scan(b("SQM", 0, 16 * QS), b("RQ", 0, 16 * QS), b("GQ", 0, 16 * QS), A.min, A.max)
        ts(b("MS", 72 * t, 72 * t + 8), b("pb7", 256, 264), 2048.0, None, A.add)
        cp(b("MS", 72 * t + 8, 72 * t + 72), b("SQM", 15, 1024, 16))
        push("m", t, b("MS", 72 * t, 72 * t + 72))
        for h in range(2):
            tt(lane("FS", h), half("FF", h), b("pb5", 64 * h, 64 * h + 64), A.add)
        push("f", t, b("FS", 128 * t, 128 * t + 128))
        if t < 3:
            mm(b("pb7", 384, 385), b("ONESF"), b("CNT"))
            cp(b("CI", 0, 1), b("pb7", 384, 385))
            ts(b("CI", 1, 2), b("CI", 0, 1), 1, None, A.bitwise_and)
            ts(b("BAR"), b("CI", 1, 2), 4.0, None, A.add)
        ml = b("ML", 72 * t, 72 * t + 72)
        arrive("p", t, b("ZW", n, n + 128))
        arrive("f", t, b("RW", n, n + 128))
        arrive("m", t, ml)
        for h in range(2):
            act(half("PB", h), b("ZW", n + h, n + 128, 2), bias=2302.75)
        B = 3856 + 64 * t
        cp(b("XT", B, B + 64), b("ML", 72 * t + 8, 72 * t + 72))
        tt(b("AF"), ind(XW, b("ML", 72 * t, 72 * t + 8)), b("PB"), A.subtract)
        if t < 3:
            ts(b("P"), b("AF"), -0.5, -1024.0, A.mult, A.add)
        else:
            for h in range(2):
                ts(b("YP", h, 128, 2), half("AF", h), -0.5, -1024.0, A.mult, A.add)
        if t == 2:
            dma("Y", "o0", T.yr[:, 0:384], T.RW[:, 768:1152], [], [b("RW", 768, 1152)])
    dma("Y", "o1", T.yr[:, 384:512], T.RW[:, 1152:1280], [], [b("RW", 1152, 1280)])
    dma("S", "o2", T.yp[:], T.YP[:], [], [b("YP")])
    for s in sorted(total):
        if clk["G"].get(s, 0) < total[s]:
            g.wait_ge(T.sem[s], total[s])
    g.wait_ge(T.sem.ls, sent[0])
